import numpy as np
CORES = [10,114,138,242]
N = 4
def setup_inputs(rng):
    return {"x": rng.standard_normal((N, 32, 1024), dtype=np.float32)}
def reference(x):
    s = x.sum(axis=0, dtype=np.float64).astype(x.dtype)
    return {"y": np.broadcast_to(s, (N,) + s.shape)}

@@ -1,0 +1,62 @@
+from concourse.bass import DstId, RemoteDMATransfer
+
+Q = 4
+W = 64
+
+SCRATCH = {
+    "s": ("sbuf", [128, Q * W], "float32"),
+    "p": ("sbuf", [128, Q * W], "float32"),
+    "r": ("sbuf", [128, Q * W], "float32"),
+}
+SEMAPHORES = ["loaded", "sent", "arrived", "result", "stored"]
+
+HELPER_OFFSET = 1
+OFF_MASKS = [0x03, 0x0C, 0x30]
+ON_MASK = 0xFF00
+FOLD_MASK = 0x00FF
+
+
+def bits(m):
+    return bin(m).count("1")
+
+
+def send_mask(i, q):
+    if i == q:
+        return ON_MASK
+    others = [k for k in range(Q) if k != i]
+    return OFF_MASKS[others.index(q)]
+
+
+def col(k):
+    return slice(k * W, (k + 1) * W)
+
+
+def rank_program(g, core, T, topo):
+    cores = list(T.cores)
+    helpers = [c + HELPER_OFFSET for c in cores]
+    rank = T.rank_of(core)
+    if rank is not None:
+        g.dma_start(T.s[:], T.x[:]).then_inc(T.sem.loaded, 16)
+        g.wait_ge(T.sem.loaded, 16)
+        trs = []
+        for q in range(Q):
+            rid, pid = topo.addr(helpers[q], core)
+            trs.append(RemoteDMATransfer(dst_ids=[DstId(rid=rid, pnc=pid)], dma_engine_mask=send_mask(rank, q),
+                                         remote_sem=T.sem.arrived, src=T.s[:, col(q)], dst=T.p[:, col(rank)]))
+        g.remote_dma_fused(trs, local_sem=T.sem.sent)
+        g.wait_ge(T.sem.result, Q * bits(FOLD_MASK))
+        g.dma_start(T.y[:], T.r[:]).then_inc(T.sem.stored, 16)
+        g.wait_ge(T.sem.sent, sum(bits(send_mask(rank, q)) for q in range(Q)))
+        g.wait_ge(T.sem.stored, 16)
+        return
+    if core in helpers:
+        q = helpers.index(core)
+        g.wait_ge(T.sem.arrived, sum(bits(send_mask(i, q)) for i in range(Q)))
+        ids = []
+        for c in cores:
+            rid, pid = topo.addr(c, core)
+            ids.append(DstId(rid=rid, pnc=pid))
+        tr = RemoteDMATransfer(dst_ids=ids, dma_engine_mask=FOLD_MASK, remote_sem=T.sem.result,
+                               srcs=[T.p[:, col(i)] for i in range(Q)], dsts=[T.r[:, col(q)] for c in cores], alu_op=1)
+        g.remote_dma_fused([tr], local_sem=T.sem.sent)
+        g.wait_ge(T.sem.sent, bits(FOLD_MASK))

@@ -4,9 +4,9 @@ Q = 4
 W = 64
 
 SCRATCH = {
-    "s": ("sbuf", [128, Q * W], "float32"),
-    "p": ("sbuf", [128, Q * W], "float32"),
-    "r": ("sbuf", [128, Q * W], "float32"),
+    "s": ("dram", [Q, 128, W], "float32"),
+    "p": ("dram", [Q, 128, W], "float32"),
+    "r": ("dram", [Q, 128, W], "float32"),
 }
 SEMAPHORES = ["loaded", "sent", "arrived", "result", "stored"]
 
@@ -27,10 +27,6 @@ def send_mask(i, q):
     return OFF_MASKS[others.index(q)]
 
 
-def col(k):
-    return slice(k * W, (k + 1) * W)
-
-
 def rank_program(g, core, T, topo):
     cores = list(T.cores)
     helpers = [c + HELPER_OFFSET for c in cores]
@@ -42,7 +38,7 @@ def rank_program(g, core, T, topo):
         for q in range(Q):
             rid, pid = topo.addr(helpers[q], core)
             trs.append(RemoteDMATransfer(dst_ids=[DstId(rid=rid, pnc=pid)], dma_engine_mask=send_mask(rank, q),
-                                         remote_sem=T.sem.arrived, src=T.s[:, col(q)], dst=T.p[:, col(rank)]))
+                                         remote_sem=T.sem.arrived, src=T.s[q], dst=T.p[rank]))
         g.remote_dma_fused(trs, local_sem=T.sem.sent)
         g.wait_ge(T.sem.result, Q * bits(FOLD_MASK))
         g.dma_start(T.y[:], T.r[:]).then_inc(T.sem.stored, 16)
@@ -57,6 +53,6 @@ def rank_program(g, core, T, topo):
             rid, pid = topo.addr(c, core)
             ids.append(DstId(rid=rid, pnc=pid))
         tr = RemoteDMATransfer(dst_ids=ids, dma_engine_mask=FOLD_MASK, remote_sem=T.sem.result,
-                               srcs=[T.p[:, col(i)] for i in range(Q)], dsts=[T.r[:, col(q)] for c in cores], alu_op=1)
+                               srcs=[T.p[i] for i in range(Q)], dsts=[T.r[q] for c in cores], alu_op=1)
         g.remote_dma_fused([tr], local_sem=T.sem.sent)
         g.wait_ge(T.sem.sent, bits(FOLD_MASK))

@@ -1,18 +1,20 @@
 from concourse.bass import DstId, RemoteDMATransfer
 
-Q = 4
-W = 64
+R = 4
+HELPER_OFFSETS = [1, 4]
+H = len(HELPER_OFFSETS)
+NP = R * H
+W = 256 // NP
 
 SCRATCH = {
-    "s": ("dram", [Q, 128, W], "float32"),
-    "p": ("dram", [Q, 128, W], "float32"),
-    "r": ("dram", [Q, 128, W], "float32"),
+    "s": ("dram", [NP, 128, W], "float32"),
+    "p": ("dram", [R, 128, W], "float32"),
+    "r": ("dram", [NP, 128, W], "float32"),
 }
 SEMAPHORES = ["loaded", "sent", "arrived", "result", "stored"]
 
-HELPER_OFFSET = 1
-OFF_MASKS = [0x03, 0x0C, 0x30]
-ON_MASK = 0xFF00
+OFF_MASKS = [0x01, 0x02, 0x04, 0x08, 0x10, 0x20]
+ON_MASKS = [0x0F00, 0xF000]
 FOLD_MASK = 0x00FF
 
 
@@ -20,39 +22,39 @@ def bits(m):
     return bin(m).count("1")
 
 
-def send_mask(i, q):
-    if i == q:
-        return ON_MASK
-    others = [k for k in range(Q) if k != i]
-    return OFF_MASKS[others.index(q)]
+def send_mask(i, k):
+    if k // H == i:
+        return ON_MASKS[k % H]
+    off = [j for j in range(NP) if j // H != i]
+    return OFF_MASKS[off.index(k)]
 
 
 def rank_program(g, core, T, topo):
     cores = list(T.cores)
-    helpers = [c + HELPER_OFFSET for c in cores]
+    helpers = [c + o for c in cores for o in HELPER_OFFSETS]
     rank = T.rank_of(core)
     if rank is not None:
         g.dma_start(T.s[:], T.x[:]).then_inc(T.sem.loaded, 16)
         g.wait_ge(T.sem.loaded, 16)
         trs = []
-        for q in range(Q):
-            rid, pid = topo.addr(helpers[q], core)
-            trs.append(RemoteDMATransfer(dst_ids=[DstId(rid=rid, pnc=pid)], dma_engine_mask=send_mask(rank, q),
-                                         remote_sem=T.sem.arrived, src=T.s[q], dst=T.p[rank]))
+        for k in range(NP):
+            rid, pid = topo.addr(helpers[k], core)
+            trs.append(RemoteDMATransfer(dst_ids=[DstId(rid=rid, pnc=pid)], dma_engine_mask=send_mask(rank, k),
+                                         remote_sem=T.sem.arrived, src=T.s[k], dst=T.p[rank]))
         g.remote_dma_fused(trs, local_sem=T.sem.sent)
-        g.wait_ge(T.sem.result, Q * bits(FOLD_MASK))
+        g.wait_ge(T.sem.result, NP * bits(FOLD_MASK))
         g.dma_start(T.y[:], T.r[:]).then_inc(T.sem.stored, 16)
-        g.wait_ge(T.sem.sent, sum(bits(send_mask(rank, q)) for q in range(Q)))
+        g.wait_ge(T.sem.sent, sum(bits(send_mask(rank, k)) for k in range(NP)))
         g.wait_ge(T.sem.stored, 16)
         return
     if core in helpers:
-        q = helpers.index(core)
-        g.wait_ge(T.sem.arrived, sum(bits(send_mask(i, q)) for i in range(Q)))
+        k = helpers.index(core)
+        g.wait_ge(T.sem.arrived, sum(bits(send_mask(i, k)) for i in range(R)))
         ids = []
         for c in cores:
             rid, pid = topo.addr(c, core)
             ids.append(DstId(rid=rid, pnc=pid))
         tr = RemoteDMATransfer(dst_ids=ids, dma_engine_mask=FOLD_MASK, remote_sem=T.sem.result,
-                               srcs=[T.p[i] for i in range(Q)], dsts=[T.r[q] for c in cores], alu_op=1)
+                               srcs=[T.p[i] for i in range(R)], dsts=[T.r[k] for c in cores], alu_op=1)
         g.remote_dma_fused([tr], local_sem=T.sem.sent)
         g.wait_ge(T.sem.sent, bits(FOLD_MASK))

@@ -1,60 +1,85 @@
 from concourse.bass import DstId, RemoteDMATransfer
 
 R = 4
-HELPER_OFFSETS = [1, 4]
-H = len(HELPER_OFFSETS)
-NP = R * H
+NP = 16
 W = 256 // NP
 
 SCRATCH = {
     "s": ("dram", [NP, 128, W], "float32"),
-    "p": ("dram", [R, 128, W], "float32"),
+    "p": ("dram", [2 * R, 128, W], "float32"),
     "r": ("dram", [NP, 128, W], "float32"),
 }
 SEMAPHORES = ["loaded", "sent", "arrived", "result", "stored"]
 
-OFF_MASKS = [0x01, 0x02, 0x04, 0x08, 0x10, 0x20]
-ON_MASKS = [0x0F00, 0xF000]
-FOLD_MASK = 0x00FF
+A_CORE = 4
+B_CORES = [1, 5]
+OFF = [[[0x03, 0x0C], [0x10, 0x20], [0x40, 0x80]],
+       [[0x01, 0x02], [0x04, 0x08], [0x30, 0xC0]]]
+ON = [0x0F00, 0xF000]
 
 
 def bits(m):
     return bin(m).count("1")
 
 
+def place(k):
+    return k // 8, (k % 8) // 2, k % 2
+
+
+def reducer(cores, k):
+    wave, q, j = place(k)
+    if wave == 0:
+        return cores[q] + A_CORE, j
+    return cores[q] + B_CORES[j], 0
+
+
 def send_mask(i, k):
-    if k // H == i:
-        return ON_MASKS[k % H]
-    off = [j for j in range(NP) if j // H != i]
-    return OFF_MASKS[off.index(k)]
+    wave, q, j = place(k)
+    if q == i:
+        return ON[j]
+    others = [(i + 1 + t) % R for t in range(R - 1)]
+    return OFF[wave][others.index(q)][j]
 
 
 def rank_program(g, core, T, topo):
     cores = list(T.cores)
-    helpers = [c + o for c in cores for o in HELPER_OFFSETS]
     rank = T.rank_of(core)
+
+    def dst_id(d):
+        rid, pid = topo.addr(d, core)
+        return DstId(rid=rid, pnc=pid)
+
     if rank is not None:
         g.dma_start(T.s[:], T.x[:]).then_inc(T.sem.loaded, 16)
         g.wait_ge(T.sem.loaded, 16)
-        trs = []
-        for k in range(NP):
-            rid, pid = topo.addr(helpers[k], core)
-            trs.append(RemoteDMATransfer(dst_ids=[DstId(rid=rid, pnc=pid)], dma_engine_mask=send_mask(rank, k),
-                                         remote_sem=T.sem.arrived, src=T.s[k], dst=T.p[rank]))
-        g.remote_dma_fused(trs, local_sem=T.sem.sent)
-        g.wait_ge(T.sem.result, NP * bits(FOLD_MASK))
+        for wave in range(2):
+            trs = []
+            for k in range(8 * wave, 8 * wave + 8):
+                h, slot = reducer(cores, k)
+                trs.append(RemoteDMATransfer(dst_ids=[dst_id(h)], dma_engine_mask=send_mask(rank, k),
+                                             remote_sem=T.sem.arrived, src=T.s[k], dst=T.p[slot * R + rank]))
+            g.remote_dma_fused(trs, local_sem=T.sem.sent)
+        g.wait_ge(T.sem.result, 8 * 4 + 8 * 8)
         g.dma_start(T.y[:], T.r[:]).then_inc(T.sem.stored, 16)
         g.wait_ge(T.sem.sent, sum(bits(send_mask(rank, k)) for k in range(NP)))
         g.wait_ge(T.sem.stored, 16)
         return
-    if core in helpers:
-        k = helpers.index(core)
-        g.wait_ge(T.sem.arrived, sum(bits(send_mask(i, k)) for i in range(R)))
-        ids = []
-        for c in cores:
-            rid, pid = topo.addr(c, core)
-            ids.append(DstId(rid=rid, pnc=pid))
-        tr = RemoteDMATransfer(dst_ids=ids, dma_engine_mask=FOLD_MASK, remote_sem=T.sem.result,
-                               srcs=[T.p[i] for i in range(R)], dsts=[T.r[k] for c in cores], alu_op=1)
-        g.remote_dma_fused([tr], local_sem=T.sem.sent)
-        g.wait_ge(T.sem.sent, bits(FOLD_MASK))
+
+    mine = [k for k in range(NP) if reducer(cores, k)[0] == core]
+    if not mine:
+        return
+    home = cores[place(mine[0])[1]]
+    away = [c for c in cores if c != home]
+    g.wait_ge(T.sem.arrived, sum(bits(send_mask(i, k)) for k in mine for i in range(R)))
+    n = 8 // len(mine)
+    trs = []
+    for t, k in enumerate(mine):
+        slot = reducer(cores, k)[1]
+        srcs = [T.p[slot * R + i] for i in range(R)]
+        m = ((1 << n) - 1) << (n * t)
+        trs.append(RemoteDMATransfer(dst_ids=[dst_id(c) for c in away], dma_engine_mask=m, remote_sem=T.sem.result,
+                                     srcs=srcs, dsts=[T.r[k] for c in away], alu_op=1))
+        trs.append(RemoteDMATransfer(dst_ids=[dst_id(home)], dma_engine_mask=m << 8, remote_sem=T.sem.result,
+                                     srcs=srcs, dsts=[T.r[k]], alu_op=1))
+    g.remote_dma_fused(trs, local_sem=T.sem.sent)
+    g.wait_ge(T.sem.sent, 16)

@@ -9,7 +9,7 @@ SCRATCH = {
     "p": ("dram", [2 * R, 128, W], "float32"),
     "r": ("dram", [NP, 128, W], "float32"),
 }
-SEMAPHORES = ["loaded", "sent", "arrived", "result", "stored"]
+SEMAPHORES = ["loaded_a", "loaded_b", "sent", "arrived", "result_a", "result_b", "stored"]
 
 A_CORE = 4
 B_CORES = [1, 5]
@@ -44,30 +44,35 @@ def send_mask(i, k):
 def rank_program(g, core, T, topo):
     cores = list(T.cores)
     rank = T.rank_of(core)
+    result = [T.sem.result_a, T.sem.result_b]
 
     def dst_id(d):
         rid, pid = topo.addr(d, core)
         return DstId(rid=rid, pnc=pid)
 
     if rank is not None:
-        g.dma_start(T.s[:], T.x[:]).then_inc(T.sem.loaded, 16)
-        g.wait_ge(T.sem.loaded, 16)
+        loaded = [T.sem.loaded_a, T.sem.loaded_b]
         for wave in range(2):
+            g.dma_start(T.s[8 * wave:8 * wave + 8], T.x[16 * wave:16 * wave + 16, :]).then_inc(loaded[wave], 16)
+        for wave in range(2):
+            g.wait_ge(loaded[wave], 16)
             trs = []
             for k in range(8 * wave, 8 * wave + 8):
                 h, slot = reducer(cores, k)
                 trs.append(RemoteDMATransfer(dst_ids=[dst_id(h)], dma_engine_mask=send_mask(rank, k),
                                              remote_sem=T.sem.arrived, src=T.s[k], dst=T.p[slot * R + rank]))
             g.remote_dma_fused(trs, local_sem=T.sem.sent)
-        g.wait_ge(T.sem.result, 8 * 4 + 8 * 8)
-        g.dma_start(T.y[:], T.r[:]).then_inc(T.sem.stored, 16)
+        for wave in range(2):
+            g.wait_ge(result[wave], 8 * (4, 8)[wave])
+            g.dma_start(T.y[16 * wave:16 * wave + 16, :], T.r[8 * wave:8 * wave + 8]).then_inc(T.sem.stored, 16)
         g.wait_ge(T.sem.sent, sum(bits(send_mask(rank, k)) for k in range(NP)))
-        g.wait_ge(T.sem.stored, 16)
+        g.wait_ge(T.sem.stored, 32)
         return
 
     mine = [k for k in range(NP) if reducer(cores, k)[0] == core]
     if not mine:
         return
+    wave = place(mine[0])[0]
     home = cores[place(mine[0])[1]]
     away = [c for c in cores if c != home]
     g.wait_ge(T.sem.arrived, sum(bits(send_mask(i, k)) for k in mine for i in range(R)))
@@ -77,9 +82,9 @@ def rank_program(g, core, T, topo):
         slot = reducer(cores, k)[1]
         srcs = [T.p[slot * R + i] for i in range(R)]
         m = ((1 << n) - 1) << (n * t)
-        trs.append(RemoteDMATransfer(dst_ids=[dst_id(c) for c in away], dma_engine_mask=m, remote_sem=T.sem.result,
+        trs.append(RemoteDMATransfer(dst_ids=[dst_id(c) for c in away], dma_engine_mask=m, remote_sem=result[wave],
                                      srcs=srcs, dsts=[T.r[k] for c in away], alu_op=1))
-        trs.append(RemoteDMATransfer(dst_ids=[dst_id(home)], dma_engine_mask=m << 8, remote_sem=T.sem.result,
+        trs.append(RemoteDMATransfer(dst_ids=[dst_id(home)], dma_engine_mask=m << 8, remote_sem=result[wave],
                                      srcs=srcs, dsts=[T.r[k]], alu_op=1))
     g.remote_dma_fused(trs, local_sem=T.sem.sent)
     g.wait_ge(T.sem.sent, 16)

from concourse.bass import DstId, RemoteDMATransfer

R = 4
NP = 16
W = 256 // NP

SCRATCH = {
    "s": ("dram", [NP, 128, W], "float32"),
    "p": ("dram", [2 * R, 128, W], "float32"),
    "r": ("dram", [NP, 128, W], "float32"),
}
SEMAPHORES = ["loaded_a", "loaded_b", "sent", "arrived", "result_a", "result_b", "stored"]

A_CORE = 4
B_CORES = [1, 5]
OFF = [[[0x03, 0x0C], [0x10, 0x20], [0x40, 0x80]],
       [[0x01, 0x02], [0x04, 0x08], [0x30, 0xC0]]]
ON = [0x0F00, 0xF000]


def bits(m):
    return bin(m).count("1")


def place(k):
    return k // 8, (k % 8) // 2, k % 2


def reducer(cores, k):
    wave, q, j = place(k)
    if wave == 0:
        return cores[q] + A_CORE, j
    return cores[q] + B_CORES[j], 0


def send_mask(i, k):
    wave, q, j = place(k)
    if q == i:
        return ON[j]
    others = [(i + 1 + t) % R for t in range(R - 1)]
    return OFF[wave][others.index(q)][j]


def rank_program(g, core, T, topo):
    cores = list(T.cores)
    rank = T.rank_of(core)
    result = [T.sem.result_a, T.sem.result_b]

    def dst_id(d):
        rid, pid = topo.addr(d, core)
        return DstId(rid=rid, pnc=pid)

    if rank is not None:
        loaded = [T.sem.loaded_a, T.sem.loaded_b]
        for wave in range(2):
            g.dma_start(T.s[8 * wave:8 * wave + 8], T.x[16 * wave:16 * wave + 16, :]).then_inc(loaded[wave], 16)
        for wave in range(2):
            g.wait_ge(loaded[wave], 16)
            trs = []
            for k in range(8 * wave, 8 * wave + 8):
                h, slot = reducer(cores, k)
                trs.append(RemoteDMATransfer(dst_ids=[dst_id(h)], dma_engine_mask=send_mask(rank, k),
                                             remote_sem=T.sem.arrived, src=T.s[k], dst=T.p[slot * R + rank]))
            g.remote_dma_fused(trs, local_sem=T.sem.sent)
        for wave in range(2):
            g.wait_ge(result[wave], 8 * (4, 8)[wave])
            g.dma_start(T.y[16 * wave:16 * wave + 16, :], T.r[8 * wave:8 * wave + 8]).then_inc(T.sem.stored, 16)
        g.wait_ge(T.sem.sent, sum(bits(send_mask(rank, k)) for k in range(NP)))
        g.wait_ge(T.sem.stored, 32)
        return

    mine = [k for k in range(NP) if reducer(cores, k)[0] == core]
    if not mine:
        return
    wave = place(mine[0])[0]
    home = cores[place(mine[0])[1]]
    away = [c for c in cores if c != home]
    g.wait_ge(T.sem.arrived, sum(bits(send_mask(i, k)) for k in mine for i in range(R)))
    n = 8 // len(mine)
    trs = []
    for t, k in enumerate(mine):
        slot = reducer(cores, k)[1]
        srcs = [T.p[slot * R + i] for i in range(R)]
        m = ((1 << n) - 1) << (n * t)
        trs.append(RemoteDMATransfer(dst_ids=[dst_id(c) for c in away], dma_engine_mask=m, remote_sem=result[wave],
                                     srcs=srcs, dsts=[T.r[k] for c in away], alu_op=1))
        trs.append(RemoteDMATransfer(dst_ids=[dst_id(home)], dma_engine_mask=m << 8, remote_sem=result[wave],
                                     srcs=srcs, dsts=[T.r[k]], alu_op=1))
    g.remote_dma_fused(trs, local_sem=T.sem.sent)
    g.wait_ge(T.sem.sent, 16)
